import numpy as np
import ml_dtypes


def mxq(x, axis, fmt="e4m3"):
    dtype, down = {"e4m3": (ml_dtypes.float8_e4m3fn, 7), "e5m2": (ml_dtypes.float8_e5m2, 14)}[fmt]
    v = np.moveaxis(np.asarray(x, np.float32).astype(ml_dtypes.bfloat16).astype(np.float64), axis, -1)
    blocks = v.reshape(v.shape[:-1] + (-1, 32))
    amax = np.abs(blocks).max(-1, keepdims=True)
    byte = np.maximum(np.where(amax > 0, np.frexp(amax)[1] - 1 + 127, 0) - down, 1)
    scale = np.exp2(byte - 127.0)
    codes = (blocks / scale).astype(np.float32).astype(dtype).astype(np.float64)
    return np.moveaxis((codes * scale).reshape(v.shape), -1, axis)


WIDE = False


def mx_kscale(k):
    if not WIDE:
        return np.ones(k)
    levels = np.array([30, -30])
    if k % 512:
        return np.exp2(np.random.permutation(np.resize(levels, k // 32))).repeat(32)
    a = np.empty((k // 512, 16))
    for p in range(k // 512):
        a[p, :8] = np.random.permutation(np.resize(levels, 8))
        for g in range(8):
            far = levels[np.abs(levels - a[p, g]) >= 10]
            a[p, g + 8] = far[np.random.randint(len(far))]
    return np.exp2(a.ravel()).repeat(32)


def f64(x):
    return np.asarray(x).astype(np.float64)


def striped(idx):
    return np.tile(np.asarray(idx).reshape(-1, 16).T, (8, 1)).astype(np.uint16)


def unstriped(offs):
    return offs[:16].T.reshape(-1).astype(np.int64)


def striped8(idx):
    return np.asarray(idx).reshape(8, -1, 16).transpose(0, 2, 1).reshape(128, -1).astype(np.uint16)


def unstriped8(offs):
    return offs.reshape(8, 16, -1).transpose(0, 2, 1).reshape(8, -1).astype(np.int64)


def pick8(x, idx, run):
    r = np.arange(len(x))
    return x[r[:, None], idx[r % (8 * run) // run]]


E2M1 = np.array([0.0, 0.5, 1.0, 1.5, 2.0, 3.0, 4.0, 6.0, -0.0, -0.5, -1.0, -1.5, -2.0, -3.0, -4.0, -6.0])


def pack_weight(w, fmt):
    k, n = w.shape
    w = f64(np.asarray(w, np.float32).astype(ml_dtypes.bfloat16)).reshape(k // 32, 32, n)
    amax = np.abs(w).max(1)
    if fmt in ("e4m3", "e5m2"):
        byte = np.frexp(amax)[1] - 1 + 127 - (7 if fmt == "e4m3" else 14)
    else:
        mant, ex = np.frexp(amax / 6.0)
        byte = np.where(mant > 0.5, ex, ex - 1) + 127
    byte = np.clip(np.where(amax > 0, byte, 1), 1, 254)
    scaled = (w * np.exp2(127.0 - byte)[:, None, :]).reshape(k, n).astype(np.float32)
    by_word = np.ascontiguousarray(scaled.reshape(k // 512, 128, 4, n).transpose(0, 1, 3, 2))
    if fmt in ("e4m3", "e5m2"):
        words = by_word.astype(ml_dtypes.float8_e4m3fn if fmt == "e4m3" else ml_dtypes.float8_e5m2).view(np.uint8)
    else:
        c = by_word.astype(ml_dtypes.float4_e2m1fn).view(np.uint8) & 0xF
        words = (c[..., 0::2] | (c[..., 1::2] << 4)).reshape(k // 512, 128, 2 * n)
    return np.ascontiguousarray(words), np.ascontiguousarray(byte.astype(np.uint8).reshape(k // 512, 16, n))


def unpack_weight(words, scales, fmt):
    g, _, n = scales.shape
    words = np.ascontiguousarray(words).reshape(g, 128, n, -1)
    if fmt in ("e4m3", "e5m2"):
        vals = words.view(ml_dtypes.float8_e4m3fn if fmt == "e4m3" else ml_dtypes.float8_e5m2).astype(np.float64)
    else:
        nib = np.empty((g, 128, n, 4), np.uint8)
        nib[..., 0::2] = words & 0xF
        nib[..., 1::2] = words >> 4
        vals = E2M1[nib]
    vals = vals * np.repeat(np.exp2(scales.astype(np.float64) - 127.0), 8, axis=1)[..., None]
    return vals.transpose(0, 1, 3, 2).reshape(g * 512, n)


K, T, J, R, C, D, I, N = 512, 1024, 256, 512, 512, 512, 256, 256


def setup_inputs():
    n = np.random.standard_normal
    idx = np.random.permutation(T)[:J]
    idx2 = np.stack([np.random.permutation(C)[:J] for _ in range(8)])
    idx3 = np.random.permutation(C)[:I]
    idx4 = np.random.permutation(C)[:I]
    idx5 = np.stack([np.random.permutation(D)[:I] for _ in range(8)])
    fk = mx_kscale(K)
    fr = mx_kscale(R)
    xtp = pack_weight(n((K, T)) / fk[:, None], "e4m3")
    wp = pack_weight(n((K, R)) * 1 / np.sqrt(K) * fk[:, None] * fr, "e2m1")
    wbp = pack_weight(n((R, N)) * 1 / np.sqrt(R) / fr[:, None], "e5m2")
    return {
        "xt_words": xtp[0],
        "xt_scales": xtp[1],
        "w_words": wp[0],
        "w_scales": wp[1],
        "wb_words": wbp[0],
        "wb_scales": wbp[1],
        "offs": striped(idx),
        "offs2": striped8(idx2),
        "offs3": striped(idx3),
        "offs4": striped(idx4),
        "offs5": striped8(idx5),
    }


def reference(xt_words, xt_scales, w_words, w_scales, wb_words, wb_scales, offs, offs2, offs3, offs4, offs5):
    idx = unstriped(offs)
    idx2 = unstriped8(offs2)
    idx3 = unstriped(offs3)
    idx4 = unstriped(offs4)
    idx5 = unstriped8(offs5)
    xtu = unpack_weight(xt_words, xt_scales, "e4m3")
    wu = unpack_weight(w_words, w_scales, "e2m1")
    wbu = unpack_weight(wb_words, wb_scales, "e5m2")
    xtidxg = xtu[:, idx]
    a = wu.T @ xtidxg
    pa = np.zeros((R, C))
    pa[np.arange(R)[:, None], idx2[np.arange(R) % 512 // 64]] = a
    h1 = np.maximum(pa[:, idx3], pa[:, idx4])
    hid = np.zeros((R, D))
    hid[np.arange(R)[:, None], idx5[np.arange(R) % 512 // 64]] = h1
    hidq = mxq(hid, 0, "e4m3")
    p = wbu.T @ hidq
    return p

@@ -1,0 +1,169 @@
+from contextlib import ExitStack
+
+import concourse.mybir as mybir
+
+K, T, J, R, C, D, I, N = 512, 1024, 256, 512, 512, 512, 256, 256
+FLOPS = 2 * K * R * J + 2 * R * N * D
+
+F32 = mybir.dt.float32
+BF16 = mybir.dt.bfloat16
+I32 = mybir.dt.int32
+U32 = mybir.dt.uint32
+U16 = mybir.dt.uint16
+U8 = mybir.dt.uint8
+E4M3 = mybir.dt.float8_e4m3fn_x4
+E5M2 = mybir.dt.float8_e5m2_x4
+E2M1 = mybir.dt.float4_e2m1fn_x4
+COPY = mybir.ActivationFunctionType.Copy
+MAX = mybir.AluOpType.max
+
+P = 128
+PACK = 4
+HALF = J // 2
+PIECE = 128
+PIECES = D // PIECE
+
+
+def tile_list_mergedstops_kernel(
+    tc, xt_words, xt_scales, w_words, w_scales, wb_words, wb_scales, offs, offs2, offs3, offs4, offs5, out
+):
+    nc = tc.nc
+    with ExitStack() as ctx:
+        lists = ctx.enter_context(tc.tile_pool(name="lists", bufs=1))
+        held = ctx.enter_context(tc.tile_pool(name="held", bufs=1))
+        boards = ctx.enter_context(tc.tile_pool(name="boards", bufs=PACK))
+        psum = ctx.enter_context(tc.psum_pool(name="psum", bufs=1))
+
+        def load_list(source, name):
+            tile = lists.tile([P, J // 16], U16, name=name)
+            nc.sync.dma_start(tile[:], source)
+            return tile
+
+        def load_scale_rows(tile, source):
+            for q in range(4):
+                nc.sync.dma_start(tile[32 * q : 32 * q + 4, :].bitcast(I32), source[0, 4 * q : 4 * q + 4, :].bitcast(I32))
+
+        xs = held.tile([P, T], U8, align_bytes=64)
+        nc.vector.memset(xs[:].bitcast(I32), 0)
+        ws = held.tile([P, R], U8, align_bytes=64)
+        nc.gpsimd.memset(ws[:].bitcast(I32), 0)
+
+        idx = load_list(offs, "idx")
+        xw = held.tile([P, T], U32, align_bytes=64)
+        nc.scalar.dma_start(xw[:].bitcast(I32), xt_words[0].rearrange("p c b -> p (c b)").bitcast(I32))
+        ww = held.tile([P, 2 * R], U8, align_bytes=64)
+        nc.sync.dma_start(ww[:].bitcast(I32), w_words[0].bitcast(I32))
+        staged = held.tile([4, 4, R // 4], I32, align_bytes=64)
+        nc.sync.dma_start(staged[:], w_scales[0].bitcast(I32).rearrange("(q r) c -> r q c", r=4))
+        load_scale_rows(xs, xt_scales)
+        idx2 = load_list(offs2, "idx2")
+        idx3 = load_list(offs3, "idx3")
+        idx4 = load_list(offs4, "idx4")
+        idx5 = load_list(offs5, "idx5")
+
+        pa = []
+        for t in range(PACK):
+            board = boards.tile([P, C], F32, name="board")
+            nc.vector.memset(board[:], 0.0)
+            pa.append(board)
+
+        nc.gpsimd.tensor_copy(ws[0:4, :].bitcast(I32), staged[:, 0, :])
+        for q in range(1, 4):
+            nc.vector.tensor_copy(ws[32 * q : 32 * q + 4, :].bitcast(I32), staged[:, q, :])
+
+        wd = []
+        wsd = []
+        for t in range(PACK):
+            dealt = held.tile([P, 2 * P], U8, align_bytes=64, name=f"wd{t}")
+            nc.scalar.copy(dealt[:].bitcast(U16), ww[:].bitcast(U16)[:, t :: PACK])
+            wd.append(dealt)
+            dealt_scales = held.tile([P, P], U8, align_bytes=64, name=f"wsd{t}")
+            nc.gpsimd.tensor_copy(dealt_scales[:], ws[:, t : R : PACK])
+            wsd.append(dealt_scales)
+
+        xg = held.tile([P, J], U32, align_bytes=64)
+        xgs = held.tile([P, J], U8, align_bytes=64)
+        for h in range(2):
+            cols = slice(h * HALF, (h + 1) * HALF)
+            part = idx[:, h * HALF // 16 : (h + 1) * HALF // 16]
+            nc.vector.tensor_copy(xgs[:, cols], xs[:].indirect(part))
+            nc.vector.tensor_copy(xg[:, cols], xw[:].indirect(part))
+
+        a = [held.tile([P, J], F32, name=f"a{t}") for t in range(PACK)]
+        steps = [(0, 0, HALF), (1, 0, HALF), (0, HALF, J), (1, HALF, J), (2, 0, J), (3, 0, J)]
+        for s, (t, j0, j1) in enumerate(steps):
+            acc = psum.tile([P, j1 - j0], F32, name=f"bank{s}")
+            nc.tensor.matmul_mx(
+                out=acc[:],
+                lhsT=wd[t][:].bitcast(E2M1),
+                lhsT_scale=wsd[t][:],
+                rhs=xg[:, j0:j1].bitcast(E4M3),
+                rhs_scale=xgs[:, j0:j1],
+                start=True,
+                stop=True,
+            )
+            if s == 0:
+                nc.scalar.activation(a[t][:, j0:j1], acc[:], COPY)
+            else:
+                nc.vector.tensor_copy(a[t][:, j0:j1], acc[:])
+            nc.scalar.activation(pa[t][:].indirect(idx2[:, j0 // 16 : j1 // 16]), a[t][:, j0:j1], COPY)
+
+        wbw = held.tile([P, N], U32, align_bytes=64)
+        nc.sync.dma_start(wbw[:].bitcast(I32), wb_words[0].rearrange("p c b -> p (c b)").bitcast(I32))
+        wbs = held.tile([P, N], U8, align_bytes=64)
+        nc.gpsimd.memset(wbs[:], 0)
+        load_scale_rows(wbs, wb_scales)
+
+        hq = [held.tile([P, PIECE, PACK], BF16, align_bytes=64, name=f"hq{c}") for c in range(PIECES)]
+        h1 = []
+        hid = []
+        for t in range(PACK):
+            first = held.tile([P, I], F32, name=f"first{t}")
+            second = held.tile([P, I], F32, name=f"second{t}")
+            larger = held.tile([P, I], F32, name=f"larger{t}")
+            nc.vector.tensor_copy(first[:], pa[t][:].indirect(idx3[:]))
+            nc.vector.tensor_copy(second[:], pa[t][:].indirect(idx4[:]))
+            board = boards.tile([P, D], F32, name="board")
+            nc.vector.memset(board[:], 0.0)
+            nc.vector.tensor_tensor(larger[:], first[:], second[:], MAX)
+            h1.append(larger)
+            hid.append(board)
+
+        def round_into(c, t):
+            nc.vector.tensor_copy(hq[c][:, :, t], hid[t][:, c * PIECE : (c + 1) * PIECE])
+
+        for t in range(PACK):
+            nc.scalar.activation(hid[t][:].indirect(idx5[:]), h1[t][:], COPY)
+            if t < PACK - 1:
+                for c in range(PIECES):
+                    round_into(c, t)
+
+        rows = out.rearrange("(m p) d -> p m d", p=P)
+        for c in range(PIECES):
+            round_into(c, PACK - 1)
+            codes = held.tile([P, PIECE], U32, align_bytes=64, name=f"codes{c}")
+            scales = held.tile([P, PIECE], U8, align_bytes=64, name=f"scales{c}")
+            nc.vector.quantize_mx(out=codes[:].bitcast(E4M3), scales=scales[:], in_=hq[c][:].rearrange("p d t -> p (d t)"))
+            result = held.tile([P, N // P, PIECE], F32, name=f"result{c}")
+            last = c == PIECES - 1
+            if last:
+                accs = [psum.tile([P, PIECE], F32, name=f"bank{c + m}")[:] for m in range(N // P)]
+            else:
+                acc = psum.tile([P, N // P, PIECE], F32, name=f"bank{c}")
+                accs = [acc[:, m, :] for m in range(N // P)]
+            for m in range(N // P):
+                nc.tensor.matmul_mx(
+                    out=accs[m],
+                    lhsT=wbw[:, m * P : (m + 1) * P].bitcast(E5M2),
+                    lhsT_scale=wbs[:, m * P : (m + 1) * P],
+                    rhs=codes[:].bitcast(E4M3),
+                    rhs_scale=scales[:],
+                    start=True,
+                    stop=True,
+                )
+            if last:
+                nc.vector.tensor_copy(result[:, 0, :], accs[0])
+                nc.scalar.activation(result[:, 1, :], accs[1], COPY)
+            else:
+                nc.scalar.activation(result[:], acc[:], COPY)
+            nc.sync.dma_start(rows[:, :, c * PIECE : (c + 1) * PIECE], result[:])

@@ -51,10 +51,10 @@ def tile_list_mergedstops_kernel(
         idx = load_list(offs, "idx")
         xw = held.tile([P, T], U32, align_bytes=64)
         nc.scalar.dma_start(xw[:].bitcast(I32), xt_words[0].rearrange("p c b -> p (c b)").bitcast(I32))
-        ww = held.tile([P, 2 * R], U8, align_bytes=64)
-        nc.sync.dma_start(ww[:].bitcast(I32), w_words[0].bitcast(I32))
         staged = held.tile([4, 4, R // 4], I32, align_bytes=64)
         nc.sync.dma_start(staged[:], w_scales[0].bitcast(I32).rearrange("(q r) c -> r q c", r=4))
+        ww = held.tile([P, 2 * R], U8, align_bytes=64)
+        nc.sync.dma_start(ww[:].bitcast(I32), w_words[0].bitcast(I32))
         load_scale_rows(xs, xt_scales)
         idx2 = load_list(offs2, "idx2")
         idx3 = load_list(offs3, "idx3")
@@ -114,7 +114,7 @@ def tile_list_mergedstops_kernel(
         nc.gpsimd.memset(wbs[:], 0)
         load_scale_rows(wbs, wb_scales)
 
-        hq = [held.tile([P, PIECE, PACK], BF16, align_bytes=64, name=f"hq{c}") for c in range(PIECES)]
+        hq = held.tile([P, D, PACK], BF16, align_bytes=64)
         h1 = []
         hid = []
         for t in range(PACK):
@@ -124,26 +124,26 @@ def tile_list_mergedstops_kernel(
             nc.vector.tensor_copy(first[:], pa[t][:].indirect(idx3[:]))
             nc.vector.tensor_copy(second[:], pa[t][:].indirect(idx4[:]))
             board = boards.tile([P, D], F32, name="board")
-            nc.vector.memset(board[:], 0.0)
+            nc.gpsimd.memset(board[:], 0.0)
             nc.vector.tensor_tensor(larger[:], first[:], second[:], MAX)
             h1.append(larger)
             hid.append(board)
 
-        def round_into(c, t):
-            nc.vector.tensor_copy(hq[c][:, :, t], hid[t][:, c * PIECE : (c + 1) * PIECE])
+        def round_into(cols, t):
+            nc.vector.tensor_copy(hq[:, cols, t], hid[t][:, cols])
 
         for t in range(PACK):
             nc.scalar.activation(hid[t][:].indirect(idx5[:]), h1[t][:], COPY)
             if t < PACK - 1:
-                for c in range(PIECES):
-                    round_into(c, t)
+                round_into(slice(0, D), t)
 
         rows = out.rearrange("(m p) d -> p m d", p=P)
         for c in range(PIECES):
-            round_into(c, PACK - 1)
+            cols = slice(c * PIECE, (c + 1) * PIECE)
+            round_into(cols, PACK - 1)
             codes = held.tile([P, PIECE], U32, align_bytes=64, name=f"codes{c}")
             scales = held.tile([P, PIECE], U8, align_bytes=64, name=f"scales{c}")
-            nc.vector.quantize_mx(out=codes[:].bitcast(E4M3), scales=scales[:], in_=hq[c][:].rearrange("p d t -> p (d t)"))
+            nc.vector.quantize_mx(out=codes[:].bitcast(E4M3), scales=scales[:], in_=hq[:, cols, :].rearrange("p d t -> p (d t)"))
             result = held.tile([P, N // P, PIECE], F32, name=f"result{c}")
             last = c == PIECES - 1
             if last:
@@ -163,7 +163,9 @@ def tile_list_mergedstops_kernel(
                 )
             if last:
                 nc.vector.tensor_copy(result[:, 0, :], accs[0])
+                nc.sync.dma_start(rows[:, 0, cols], result[:, 0, :])
                 nc.scalar.activation(result[:, 1, :], accs[1], COPY)
+                nc.scalar.dma_start(rows[:, 1, cols], result[:, 1, :])
             else:
                 nc.scalar.activation(result[:], acc[:], COPY)
-            nc.sync.dma_start(rows[:, :, c * PIECE : (c + 1) * PIECE], result[:])
+                nc.sync.dma_start(rows[:, :, cols], result[:])

@@ -31,7 +31,6 @@ def tile_list_mergedstops_kernel(
     with ExitStack() as ctx:
         lists = ctx.enter_context(tc.tile_pool(name="lists", bufs=1))
         held = ctx.enter_context(tc.tile_pool(name="held", bufs=1))
-        boards = ctx.enter_context(tc.tile_pool(name="boards", bufs=PACK))
         psum = ctx.enter_context(tc.psum_pool(name="psum", bufs=1))
 
         def load_list(source, name):
@@ -63,7 +62,7 @@ def tile_list_mergedstops_kernel(
 
         pa = []
         for t in range(PACK):
-            board = boards.tile([P, C], F32, name="board")
+            board = held.tile([P, C], F32, align_bytes=64, name=f"pa{t}", tag=f"pa{t}")
             nc.vector.memset(board[:], 0.0)
             pa.append(board)
 
@@ -72,14 +71,13 @@ def tile_list_mergedstops_kernel(
             nc.vector.tensor_copy(ws[32 * q : 32 * q + 4, :].bitcast(I32), staged[:, q, :])
 
         wd = []
-        wsd = []
+        wsd = [held.tile([P, 2, P], U8, align_bytes=64, name=f"wsd{u}") for u in range(2)]
+        by_slot = ws[:].rearrange("p (q t) -> p t q", t=PACK)
+        nc.vector.tensor_copy(wsd[0][:], by_slot[:, 0:2, :])
         for t in range(PACK):
-            dealt = held.tile([P, 2 * P], U8, align_bytes=64, name=f"wd{t}")
+            dealt = held.tile([P, 2 * P], U8, align_bytes=64, name=f"wd{t}", tag=f"wd{t}")
             nc.scalar.copy(dealt[:].bitcast(U16), ww[:].bitcast(U16)[:, t :: PACK])
             wd.append(dealt)
-            dealt_scales = held.tile([P, P], U8, align_bytes=64, name=f"wsd{t}")
-            nc.gpsimd.tensor_copy(dealt_scales[:], ws[:, t : R : PACK])
-            wsd.append(dealt_scales)
 
         xg = held.tile([P, J], U32, align_bytes=64)
         xgs = held.tile([P, J], U8, align_bytes=64)
@@ -88,6 +86,7 @@ def tile_list_mergedstops_kernel(
             part = idx[:, h * HALF // 16 : (h + 1) * HALF // 16]
             nc.vector.tensor_copy(xgs[:, cols], xs[:].indirect(part))
             nc.vector.tensor_copy(xg[:, cols], xw[:].indirect(part))
+        nc.vector.tensor_copy(wsd[1][:], by_slot[:, 2:4, :])
 
         a = [held.tile([P, J], F32, name=f"a{t}") for t in range(PACK)]
         steps = [(0, 0, HALF), (1, 0, HALF), (0, HALF, J), (1, HALF, J), (2, 0, J), (3, 0, J)]
@@ -96,7 +95,7 @@ def tile_list_mergedstops_kernel(
             nc.tensor.matmul_mx(
                 out=acc[:],
                 lhsT=wd[t][:].bitcast(E2M1),
-                lhsT_scale=wsd[t][:],
+                lhsT_scale=wsd[t // 2][:, t % 2, :],
                 rhs=xg[:, j0:j1].bitcast(E4M3),
                 rhs_scale=xgs[:, j0:j1],
                 start=True,
@@ -108,26 +107,29 @@ def tile_list_mergedstops_kernel(
                 nc.vector.tensor_copy(a[t][:, j0:j1], acc[:])
             nc.scalar.activation(pa[t][:].indirect(idx2[:, j0 // 16 : j1 // 16]), a[t][:, j0:j1], COPY)
 
+        hid = []
+        for t in range(PACK):
+            board = held.tile([P, D], F32, align_bytes=64, name=f"hid{t}", tag=f"wd{t}")
+            nc.vector.memset(board[:], 0.0)
+            hid.append(board)
+
         wbw = held.tile([P, N], U32, align_bytes=64)
         nc.sync.dma_start(wbw[:].bitcast(I32), wb_words[0].rearrange("p c b -> p (c b)").bitcast(I32))
         wbs = held.tile([P, N], U8, align_bytes=64)
         nc.gpsimd.memset(wbs[:], 0)
         load_scale_rows(wbs, wb_scales)
 
-        hq = held.tile([P, D, PACK], BF16, align_bytes=64)
         h1 = []
-        hid = []
         for t in range(PACK):
             first = held.tile([P, I], F32, name=f"first{t}")
             second = held.tile([P, I], F32, name=f"second{t}")
             larger = held.tile([P, I], F32, name=f"larger{t}")
             nc.vector.tensor_copy(first[:], pa[t][:].indirect(idx3[:]))
             nc.vector.tensor_copy(second[:], pa[t][:].indirect(idx4[:]))
-            board = boards.tile([P, D], F32, name="board")
-            nc.gpsimd.memset(board[:], 0.0)
             nc.vector.tensor_tensor(larger[:], first[:], second[:], MAX)
             h1.append(larger)
-            hid.append(board)
+
+        hq = held.tile([P, D, PACK], BF16, align_bytes=64, tag=f"pa{PACK - 1}")
 
         def round_into(cols, t):
             nc.vector.tensor_copy(hq[:, cols, t], hid[t][:, cols])

@@ -42,18 +42,18 @@ def tile_list_mergedstops_kernel(
             for q in range(4):
                 nc.sync.dma_start(tile[32 * q : 32 * q + 4, :].bitcast(I32), source[0, 4 * q : 4 * q + 4, :].bitcast(I32))
 
-        xs = held.tile([P, T], U8, align_bytes=64)
+        xs = held.tile([P, T], U8, align_bytes=64, tag="xs")
         nc.vector.memset(xs[:].bitcast(I32), 0)
         ws = held.tile([P, R], U8, align_bytes=64)
         nc.gpsimd.memset(ws[:].bitcast(I32), 0)
 
-        idx = load_list(offs, "idx")
-        xw = held.tile([P, T], U32, align_bytes=64)
-        nc.scalar.dma_start(xw[:].bitcast(I32), xt_words[0].rearrange("p c b -> p (c b)").bitcast(I32))
         staged = held.tile([4, 4, R // 4], I32, align_bytes=64)
         nc.sync.dma_start(staged[:], w_scales[0].bitcast(I32).rearrange("(q r) c -> r q c", r=4))
         ww = held.tile([P, 2 * R], U8, align_bytes=64)
-        nc.sync.dma_start(ww[:].bitcast(I32), w_words[0].bitcast(I32))
+        nc.scalar.dma_start(ww[:].bitcast(I32), w_words[0].bitcast(I32))
+        idx = load_list(offs, "idx")
+        xw = held.tile([P, T], U32, align_bytes=64)
+        nc.sync.dma_start(xw[:].bitcast(I32), xt_words[0].rearrange("p c b -> p (c b)").bitcast(I32))
         load_scale_rows(xs, xt_scales)
         idx2 = load_list(offs2, "idx2")
         idx3 = load_list(offs3, "idx3")
@@ -79,28 +79,31 @@ def tile_list_mergedstops_kernel(
             nc.scalar.copy(dealt[:].bitcast(U16), ww[:].bitcast(U16)[:, t :: PACK])
             wd.append(dealt)
 
-        xg = held.tile([P, J], U32, align_bytes=64)
         xgs = held.tile([P, J], U8, align_bytes=64)
+        xg = []
         for h in range(2):
-            cols = slice(h * HALF, (h + 1) * HALF)
             part = idx[:, h * HALF // 16 : (h + 1) * HALF // 16]
-            nc.vector.tensor_copy(xgs[:, cols], xs[:].indirect(part))
-            nc.vector.tensor_copy(xg[:, cols], xw[:].indirect(part))
+            nc.vector.tensor_copy(xgs[:, h * HALF : (h + 1) * HALF], xs[:].indirect(part))
+            words = held.tile([P, HALF], U32, align_bytes=64, name=f"xg{h}", tag=("xg", "xs")[h])
+            nc.vector.tensor_copy(words[:], xw[:].indirect(part))
+            xg.append(words)
         nc.vector.tensor_copy(wsd[1][:], by_slot[:, 2:4, :])
 
         a = [held.tile([P, J], F32, name=f"a{t}") for t in range(PACK)]
-        steps = [(0, 0, HALF), (1, 0, HALF), (0, HALF, J), (1, HALF, J), (2, 0, J), (3, 0, J)]
-        for s, (t, j0, j1) in enumerate(steps):
+        steps = [(0, [0]), (1, [0]), (0, [1]), (1, [1]), (2, [0, 1]), (3, [0, 1])]
+        for s, (t, halves) in enumerate(steps):
+            j0, j1 = halves[0] * HALF, (halves[-1] + 1) * HALF
             acc = psum.tile([P, j1 - j0], F32, name=f"bank{s}")
-            nc.tensor.matmul_mx(
-                out=acc[:],
-                lhsT=wd[t][:].bitcast(E2M1),
-                lhsT_scale=wsd[t // 2][:, t % 2, :],
-                rhs=xg[:, j0:j1].bitcast(E4M3),
-                rhs_scale=xgs[:, j0:j1],
-                start=True,
-                stop=True,
-            )
+            for h in halves:
+                nc.tensor.matmul_mx(
+                    out=acc[:, h * HALF - j0 : (h + 1) * HALF - j0],
+                    lhsT=wd[t][:].bitcast(E2M1),
+                    lhsT_scale=wsd[t // 2][:, t % 2, :],
+                    rhs=xg[h][:].bitcast(E4M3),
+                    rhs_scale=xgs[:, h * HALF : (h + 1) * HALF],
+                    start=True,
+                    stop=True,
+                )
             if s == 0:
                 nc.scalar.activation(a[t][:, j0:j1], acc[:], COPY)
             else:

@@ -22,6 +22,7 @@ PACK = 4
 HALF = J // 2
 PIECE = 128
 PIECES = D // PIECE
+ORDER = (2, 0, 1, 3)
 
 
 def tile_list_mergedstops_kernel(
@@ -60,24 +61,24 @@ def tile_list_mergedstops_kernel(
         idx4 = load_list(offs4, "idx4")
         idx5 = load_list(offs5, "idx5")
 
-        pa = []
-        for t in range(PACK):
+        pa = {}
+        for t in ORDER:
             board = held.tile([P, C], F32, align_bytes=64, name=f"pa{t}", tag=f"pa{t}")
             nc.vector.memset(board[:], 0.0)
-            pa.append(board)
+            pa[t] = board
 
         nc.gpsimd.tensor_copy(ws[0:4, :].bitcast(I32), staged[:, 0, :])
         for q in range(1, 4):
             nc.vector.tensor_copy(ws[32 * q : 32 * q + 4, :].bitcast(I32), staged[:, q, :])
 
-        wd = []
+        wd = {}
         wsd = [held.tile([P, 2, P], U8, align_bytes=64, name=f"wsd{u}") for u in range(2)]
         by_slot = ws[:].rearrange("p (q t) -> p t q", t=PACK)
-        nc.vector.tensor_copy(wsd[0][:], by_slot[:, 0:2, :])
-        for t in range(PACK):
+        nc.vector.tensor_copy(wsd[0][:], by_slot[:, 0::2, :])
+        for t in ORDER:
             dealt = held.tile([P, 2 * P], U8, align_bytes=64, name=f"wd{t}", tag=f"wd{t}")
             nc.scalar.copy(dealt[:].bitcast(U16), ww[:].bitcast(U16)[:, t :: PACK])
-            wd.append(dealt)
+            wd[t] = dealt
 
         xgs = held.tile([P, J], U8, align_bytes=64)
         xg = []
@@ -87,10 +88,10 @@ def tile_list_mergedstops_kernel(
             words = held.tile([P, HALF], U32, align_bytes=64, name=f"xg{h}", tag=("xg", "xs")[h])
             nc.vector.tensor_copy(words[:], xw[:].indirect(part))
             xg.append(words)
-        nc.vector.tensor_copy(wsd[1][:], by_slot[:, 2:4, :])
+        nc.vector.tensor_copy(wsd[1][:], by_slot[:, 1::2, :])
 
         a = [held.tile([P, J], F32, name=f"a{t}") for t in range(PACK)]
-        steps = [(0, [0]), (1, [0]), (0, [1]), (1, [1]), (2, [0, 1]), (3, [0, 1])]
+        steps = [(t, [h]) for h in range(2) for t in ORDER[:2]] + [(t, [0, 1]) for t in ORDER[2:]]
         for s, (t, halves) in enumerate(steps):
             j0, j1 = halves[0] * HALF, (halves[-1] + 1) * HALF
             acc = psum.tile([P, j1 - j0], F32, name=f"bank{s}")
@@ -98,7 +99,7 @@ def tile_list_mergedstops_kernel(
                 nc.tensor.matmul_mx(
                     out=acc[:, h * HALF - j0 : (h + 1) * HALF - j0],
                     lhsT=wd[t][:].bitcast(E2M1),
-                    lhsT_scale=wsd[t // 2][:, t % 2, :],
+                    lhsT_scale=wsd[t % 2][:, t // 2, :],
                     rhs=xg[h][:].bitcast(E4M3),
                     rhs_scale=xgs[:, h * HALF : (h + 1) * HALF],
                     start=True,
@@ -110,11 +111,14 @@ def tile_list_mergedstops_kernel(
                 nc.vector.tensor_copy(a[t][:, j0:j1], acc[:])
             nc.scalar.activation(pa[t][:].indirect(idx2[:, j0 // 16 : j1 // 16]), a[t][:, j0:j1], COPY)
 
-        hid = []
-        for t in range(PACK):
-            board = held.tile([P, D], F32, align_bytes=64, name=f"hid{t}", tag=f"wd{t}")
-            nc.vector.memset(board[:], 0.0)
-            hid.append(board)
+        hid = {}
+
+        def clear_board(t, tag):
+            hid[t] = held.tile([P, D], F32, align_bytes=64, name=f"hid{t}", tag=tag)
+            nc.vector.memset(hid[t][:], 0.0)
+
+        for t in ORDER[:-1]:
+            clear_board(t, f"wd{t}")
 
         wbw = held.tile([P, N], U32, align_bytes=64)
         nc.sync.dma_start(wbw[:].bitcast(I32), wb_words[0].rearrange("p c b -> p (c b)").bitcast(I32))
@@ -122,30 +126,34 @@ def tile_list_mergedstops_kernel(
         nc.gpsimd.memset(wbs[:], 0)
         load_scale_rows(wbs, wb_scales)
 
-        h1 = []
-        for t in range(PACK):
+        h1 = {}
+        for t in ORDER:
             first = held.tile([P, I], F32, name=f"first{t}")
             second = held.tile([P, I], F32, name=f"second{t}")
             larger = held.tile([P, I], F32, name=f"larger{t}")
             nc.vector.tensor_copy(first[:], pa[t][:].indirect(idx3[:]))
             nc.vector.tensor_copy(second[:], pa[t][:].indirect(idx4[:]))
             nc.vector.tensor_tensor(larger[:], first[:], second[:], MAX)
-            h1.append(larger)
+            h1[t] = larger
 
         hq = held.tile([P, D, PACK], BF16, align_bytes=64, tag=f"pa{PACK - 1}")
 
-        def round_into(cols, t):
-            nc.vector.tensor_copy(hq[:, cols, t], hid[t][:, cols])
-
-        for t in range(PACK):
+        for t in ORDER:
             nc.scalar.activation(hid[t][:].indirect(idx5[:]), h1[t][:], COPY)
-            if t < PACK - 1:
-                round_into(slice(0, D), t)
+            if t != ORDER[-1]:
+                nc.vector.tensor_copy(hq[:, :, t], hid[t][:])
+            if t == ORDER[0]:
+                clear_board(ORDER[-1], f"wd{t}")
+        t = ORDER[-1]
+        for c in range(1, PIECES, 2):
+            cols = slice(c * PIECE, (c + 1) * PIECE)
+            nc.scalar.copy(hq[:, cols, t], hid[t][:, cols])
 
         rows = out.rearrange("(m p) d -> p m d", p=P)
         for c in range(PIECES):
             cols = slice(c * PIECE, (c + 1) * PIECE)
-            round_into(cols, PACK - 1)
+            if c % 2 == 0:
+                nc.vector.tensor_copy(hq[:, cols, t], hid[t][:, cols])
             codes = held.tile([P, PIECE], U32, align_bytes=64, name=f"codes{c}")
             scales = held.tile([P, PIECE], U8, align_bytes=64, name=f"scales{c}")
             nc.vector.quantize_mx(out=codes[:].bitcast(E4M3), scales=scales[:], in_=hq[:, cols, :].rearrange("p d t -> p (d t)"))

from contextlib import ExitStack

import concourse.mybir as mybir

K, T, J, R, C, D, I, N = 512, 1024, 256, 512, 512, 512, 256, 256
FLOPS = 2 * K * R * J + 2 * R * N * D

F32 = mybir.dt.float32
BF16 = mybir.dt.bfloat16
I32 = mybir.dt.int32
U32 = mybir.dt.uint32
U16 = mybir.dt.uint16
U8 = mybir.dt.uint8
E4M3 = mybir.dt.float8_e4m3fn_x4
E5M2 = mybir.dt.float8_e5m2_x4
E2M1 = mybir.dt.float4_e2m1fn_x4
COPY = mybir.ActivationFunctionType.Copy
MAX = mybir.AluOpType.max

P = 128
PACK = 4
HALF = J // 2
PIECE = 128
PIECES = D // PIECE
ORDER = (2, 0, 1, 3)


def tile_list_mergedstops_kernel(
    tc, xt_words, xt_scales, w_words, w_scales, wb_words, wb_scales, offs, offs2, offs3, offs4, offs5, out
):
    nc = tc.nc
    with ExitStack() as ctx:
        lists = ctx.enter_context(tc.tile_pool(name="lists", bufs=1))
        held = ctx.enter_context(tc.tile_pool(name="held", bufs=1))
        psum = ctx.enter_context(tc.psum_pool(name="psum", bufs=1))

        def load_list(source, name):
            tile = lists.tile([P, J // 16], U16, name=name)
            nc.sync.dma_start(tile[:], source)
            return tile

        def load_scale_rows(tile, source):
            for q in range(4):
                nc.sync.dma_start(tile[32 * q : 32 * q + 4, :].bitcast(I32), source[0, 4 * q : 4 * q + 4, :].bitcast(I32))

        xs = held.tile([P, T], U8, align_bytes=64, tag="xs")
        nc.vector.memset(xs[:].bitcast(I32), 0)
        ws = held.tile([P, R], U8, align_bytes=64)
        nc.gpsimd.memset(ws[:].bitcast(I32), 0)

        staged = held.tile([4, 4, R // 4], I32, align_bytes=64)
        nc.sync.dma_start(staged[:], w_scales[0].bitcast(I32).rearrange("(q r) c -> r q c", r=4))
        ww = held.tile([P, 2 * R], U8, align_bytes=64)
        nc.scalar.dma_start(ww[:].bitcast(I32), w_words[0].bitcast(I32))
        idx = load_list(offs, "idx")
        xw = held.tile([P, T], U32, align_bytes=64)
        nc.sync.dma_start(xw[:].bitcast(I32), xt_words[0].rearrange("p c b -> p (c b)").bitcast(I32))
        load_scale_rows(xs, xt_scales)
        idx2 = load_list(offs2, "idx2")
        idx3 = load_list(offs3, "idx3")
        idx4 = load_list(offs4, "idx4")
        idx5 = load_list(offs5, "idx5")

        pa = {}
        for t in ORDER:
            board = held.tile([P, C], F32, align_bytes=64, name=f"pa{t}", tag=f"pa{t}")
            nc.vector.memset(board[:], 0.0)
            pa[t] = board

        nc.gpsimd.tensor_copy(ws[0:4, :].bitcast(I32), staged[:, 0, :])
        for q in range(1, 4):
            nc.vector.tensor_copy(ws[32 * q : 32 * q + 4, :].bitcast(I32), staged[:, q, :])

        wd = {}
        wsd = [held.tile([P, 2, P], U8, align_bytes=64, name=f"wsd{u}") for u in range(2)]
        by_slot = ws[:].rearrange("p (q t) -> p t q", t=PACK)
        nc.vector.tensor_copy(wsd[0][:], by_slot[:, 0::2, :])
        for t in ORDER:
            dealt = held.tile([P, 2 * P], U8, align_bytes=64, name=f"wd{t}", tag=f"wd{t}")
            nc.scalar.copy(dealt[:].bitcast(U16), ww[:].bitcast(U16)[:, t :: PACK])
            wd[t] = dealt

        xgs = held.tile([P, J], U8, align_bytes=64)
        xg = []
        for h in range(2):
            part = idx[:, h * HALF // 16 : (h + 1) * HALF // 16]
            nc.vector.tensor_copy(xgs[:, h * HALF : (h + 1) * HALF], xs[:].indirect(part))
            words = held.tile([P, HALF], U32, align_bytes=64, name=f"xg{h}", tag=("xg", "xs")[h])
            nc.vector.tensor_copy(words[:], xw[:].indirect(part))
            xg.append(words)
        nc.vector.tensor_copy(wsd[1][:], by_slot[:, 1::2, :])

        a = [held.tile([P, J], F32, name=f"a{t}") for t in range(PACK)]
        steps = [(t, [h]) for h in range(2) for t in ORDER[:2]] + [(t, [0, 1]) for t in ORDER[2:]]
        for s, (t, halves) in enumerate(steps):
            j0, j1 = halves[0] * HALF, (halves[-1] + 1) * HALF
            acc = psum.tile([P, j1 - j0], F32, name=f"bank{s}")
            for h in halves:
                nc.tensor.matmul_mx(
                    out=acc[:, h * HALF - j0 : (h + 1) * HALF - j0],
                    lhsT=wd[t][:].bitcast(E2M1),
                    lhsT_scale=wsd[t % 2][:, t // 2, :],
                    rhs=xg[h][:].bitcast(E4M3),
                    rhs_scale=xgs[:, h * HALF : (h + 1) * HALF],
                    start=True,
                    stop=True,
                )
            if s == 0:
                nc.scalar.activation(a[t][:, j0:j1], acc[:], COPY)
            else:
                nc.vector.tensor_copy(a[t][:, j0:j1], acc[:])
            nc.scalar.activation(pa[t][:].indirect(idx2[:, j0 // 16 : j1 // 16]), a[t][:, j0:j1], COPY)

        hid = {}

        def clear_board(t, tag):
            hid[t] = held.tile([P, D], F32, align_bytes=64, name=f"hid{t}", tag=tag)
            nc.vector.memset(hid[t][:], 0.0)

        for t in ORDER[:-1]:
            clear_board(t, f"wd{t}")

        wbw = held.tile([P, N], U32, align_bytes=64)
        nc.sync.dma_start(wbw[:].bitcast(I32), wb_words[0].rearrange("p c b -> p (c b)").bitcast(I32))
        wbs = held.tile([P, N], U8, align_bytes=64)
        nc.gpsimd.memset(wbs[:], 0)
        load_scale_rows(wbs, wb_scales)

        h1 = {}
        for t in ORDER:
            first = held.tile([P, I], F32, name=f"first{t}")
            second = held.tile([P, I], F32, name=f"second{t}")
            larger = held.tile([P, I], F32, name=f"larger{t}")
            nc.vector.tensor_copy(first[:], pa[t][:].indirect(idx3[:]))
            nc.vector.tensor_copy(second[:], pa[t][:].indirect(idx4[:]))
            nc.vector.tensor_tensor(larger[:], first[:], second[:], MAX)
            h1[t] = larger

        hq = held.tile([P, D, PACK], BF16, align_bytes=64, tag=f"pa{PACK - 1}")

        for t in ORDER:
            nc.scalar.activation(hid[t][:].indirect(idx5[:]), h1[t][:], COPY)
            if t != ORDER[-1]:
                nc.vector.tensor_copy(hq[:, :, t], hid[t][:])
            if t == ORDER[0]:
                clear_board(ORDER[-1], f"wd{t}")
        t = ORDER[-1]
        for c in range(1, PIECES, 2):
            cols = slice(c * PIECE, (c + 1) * PIECE)
            nc.scalar.copy(hq[:, cols, t], hid[t][:, cols])

        rows = out.rearrange("(m p) d -> p m d", p=P)
        for c in range(PIECES):
            cols = slice(c * PIECE, (c + 1) * PIECE)
            if c % 2 == 0:
                nc.vector.tensor_copy(hq[:, cols, t], hid[t][:, cols])
            codes = held.tile([P, PIECE], U32, align_bytes=64, name=f"codes{c}")
            scales = held.tile([P, PIECE], U8, align_bytes=64, name=f"scales{c}")
            nc.vector.quantize_mx(out=codes[:].bitcast(E4M3), scales=scales[:], in_=hq[:, cols, :].rearrange("p d t -> p (d t)"))
            result = held.tile([P, N // P, PIECE], F32, name=f"result{c}")
            last = c == PIECES - 1
            if last:
                accs = [psum.tile([P, PIECE], F32, name=f"bank{c + m}")[:] for m in range(N // P)]
            else:
                acc = psum.tile([P, N // P, PIECE], F32, name=f"bank{c}")
                accs = [acc[:, m, :] for m in range(N // P)]
            for m in range(N // P):
                nc.tensor.matmul_mx(
                    out=accs[m],
                    lhsT=wbw[:, m * P : (m + 1) * P].bitcast(E5M2),
                    lhsT_scale=wbs[:, m * P : (m + 1) * P],
                    rhs=codes[:].bitcast(E4M3),
                    rhs_scale=scales[:],
                    start=True,
                    stop=True,
                )
            if last:
                nc.vector.tensor_copy(result[:, 0, :], accs[0])
                nc.sync.dma_start(rows[:, 0, cols], result[:, 0, :])
                nc.scalar.activation(result[:, 1, :], accs[1], COPY)
                nc.scalar.dma_start(rows[:, 1, cols], result[:, 1, :])
            else:
                nc.scalar.activation(result[:], acc[:], COPY)
                nc.sync.dma_start(rows[:, :, cols], result[:])
